import numpy as np
import ml_dtypes


def mxq(x, axis, fmt="e4m3"):
    dtype, down = {"e4m3": (ml_dtypes.float8_e4m3fn, 7), "e5m2": (ml_dtypes.float8_e5m2, 14)}[fmt]
    v = np.moveaxis(np.asarray(x, np.float32).astype(ml_dtypes.bfloat16).astype(np.float64), axis, -1)
    blocks = v.reshape(v.shape[:-1] + (-1, 32))
    amax = np.abs(blocks).max(-1, keepdims=True)
    byte = np.maximum(np.where(amax > 0, np.frexp(amax)[1] - 1 + 127, 0) - down, 1)
    scale = np.exp2(byte - 127.0)
    codes = (blocks / scale).astype(np.float32).astype(dtype).astype(np.float64)
    return np.moveaxis((codes * scale).reshape(v.shape), -1, axis)


WIDE = False


def mx_kscale(k):
    if not WIDE:
        return np.ones(k)
    levels = np.array([10, -10, 5, -5, 0])
    if k % 512:
        return np.exp2(np.random.permutation(np.resize(levels, k // 32))).repeat(32)
    a = np.empty((k // 512, 16))
    for p in range(k // 512):
        a[p, :8] = np.random.permutation(np.resize(levels, 8))
        for g in range(8):
            far = levels[np.abs(levels - a[p, g]) >= 10]
            a[p, g + 8] = far[np.random.randint(len(far))]
    return np.exp2(a.ravel()).repeat(32)


BF16 = ml_dtypes.bfloat16


def bf(x):
    return np.asarray(x, np.float32).astype(BF16)


def f64(x):
    return np.asarray(x).astype(np.float64)


E2M1 = np.array([0.0, 0.5, 1.0, 1.5, 2.0, 3.0, 4.0, 6.0, -0.0, -0.5, -1.0, -1.5, -2.0, -3.0, -4.0, -6.0])


def pack_weight(w, fmt):
    k, n = w.shape
    w = f64(bf(w)).reshape(k // 32, 32, n)
    amax = np.abs(w).max(1)
    if fmt == "e4m3":
        byte = np.frexp(amax)[1] - 1 + 127 - 7
    else:
        mant, ex = np.frexp(amax / 6.0)
        byte = np.where(mant > 0.5, ex, ex - 1) + 127
    byte = np.clip(np.where(amax > 0, byte, 1), 1, 254)
    scaled = (w * np.exp2(127.0 - byte)[:, None, :]).reshape(k, n).astype(np.float32)
    by_word = np.ascontiguousarray(scaled.reshape(k // 512, 128, 4, n).transpose(0, 1, 3, 2))
    if fmt == "e4m3":
        words = by_word.astype(ml_dtypes.float8_e4m3fn).view(np.uint8)
    else:
        c = by_word.astype(ml_dtypes.float4_e2m1fn).view(np.uint8) & 0xF
        words = c[..., 0::2] | (c[..., 1::2] << 4)
    return np.ascontiguousarray(words), np.ascontiguousarray(byte.astype(np.uint8).reshape(k // 512, 16, n))


def unpack_weight(words, scales, fmt):
    g, p, n, _ = words.shape
    if fmt == "e4m3":
        vals = np.ascontiguousarray(words).view(ml_dtypes.float8_e4m3fn).astype(np.float64)
    else:
        nib = np.empty((g, p, n, 4), np.uint8)
        nib[..., 0::2] = words & 0xF
        nib[..., 1::2] = words >> 4
        vals = E2M1[nib]
    vals = vals * np.repeat(np.exp2(scales.astype(np.float64) - 127.0), 8, axis=1)[..., None]
    return vals.transpose(0, 1, 3, 2).reshape(g * 512, n)
def pack4(w):
    words, scales = pack_weight(w, "e2m1")
    return words.reshape(words.shape[0], 128, -1), scales


def unpack4(words, scales):
    return unpack_weight(words.reshape(words.shape[0], 128, -1, 2), scales, "e2m1")


T, DI, DO, R = 2048, 1024, 1024, 256


def draw0():
    s, t = mx_kscale(T), mx_kscale(DO)
    x = bf((0.3 + np.random.standard_normal((T, DI))) * s[:, None])
    g = bf(np.random.standard_normal((T, DO)) / np.sqrt(T) / s[:, None])
    v = bf((0.5 + np.random.standard_normal((DI, DO))) / np.sqrt(DI))
    m = bf((1.0 + 0.1 * np.random.standard_normal(DO)) * t)
    b = np.random.standard_normal((R, DO)) / np.sqrt(DO) / t[None, :]
    b_words, b_scales = pack4(b.T)
    return {"x": x, "g": g, "v": v, "m": m, "b_words": b_words, "b_scales": b_scales}


def unit_columns(v):
    n = np.sqrt(np.sum(v * v, axis=0))
    u = v / n[None, :]
    return n, u


def core(x, g, v, m, b_words, b_scales):
    n, u = unit_columns(f64(v))
    gw = mxq(f64(x), 0, "e4m3").T @ mxq(f64(g), 0, "e4m3")
    c = np.sum(u * gw, axis=0)
    dv = (f64(m) / n)[None, :] * (gw - u * c[None, :])
    return mxq(dv, 1, "e4m3") @ unpack4(b_words, b_scales)


def e4m3fn_bytes(y):
    return np.clip(np.asarray(y, np.float64), -448.0, 448.0).astype(np.float32).astype(ml_dtypes.float8_e4m3fn).view(np.uint8)


def e4m3fn_values(b):
    return np.asarray(b, np.uint8).view(ml_dtypes.float8_e4m3fn).astype(np.float64)


def setup_inputs():
    d = draw0()
    x0 = np.asarray(d['x']).astype(np.float64)
    s = (np.max(np.abs(x0), axis=(1,), keepdims=True) / 448.0).astype(np.float32)
    out = {}
    for k, v in d.items():
        if k == 'x':
            out['x_bytes'] = e4m3fn_bytes(x0 / s.astype(np.float64))
            out['x_scale'] = s
        else:
            out[k] = v
    return out


def reference(x_bytes, x_scale, g, v, m, b_words, b_scales):
    return core(e4m3fn_values(x_bytes) * x_scale.astype(np.float64), g, v, m, b_words, b_scales)

@@ -1,0 +1,366 @@
+from contextlib import ExitStack
+
+import concourse.mybir as mybir
+from concourse.masks import make_identity
+
+T, DI, DO, R = 2048, 1024, 1024, 256
+FLOPS = 2 * T * DI * DO + 2 * DI * DO * R
+
+P = 128
+F32 = mybir.dt.float32
+BF16 = mybir.dt.bfloat16
+I32 = mybir.dt.int32
+U32 = mybir.dt.uint32
+U8 = mybir.dt.uint8
+FP8 = mybir.dt.float8_e4m3fn
+E4M3X4 = mybir.dt.float8_e4m3fn_x4
+E2M1X4 = mybir.dt.float4_e2m1fn_x4
+ACT = mybir.ActivationFunctionType
+ALU = mybir.AluOpType
+
+NQ = T // 512
+NG = DO // 512
+HALF = 512
+
+SCALAR_WIDENS = {0: (3,), 1: (2, 3), 2: (2, 3), 3: (2, 3)}
+
+
+def tile_doradirectiongradienttoloradown_w4_kernel(tc, x_bytes, x_scale, g, v, m, b_words, b_scales, out):
+    nc = tc.nc
+    with ExitStack() as ctx:
+        keep = ctx.enter_context(tc.tile_pool(name="keep", bufs=1))
+        work = ctx.enter_context(tc.tile_pool(name="work", bufs=2))
+        psum = ctx.enter_context(tc.psum_pool(name="psum", bufs=1))
+        ctx.enter_context(tc.manual_schedule())
+
+        def kt(shape, dtype, name):
+            t = keep.tile(shape, dtype, name=name, align_bytes=64)
+            return t
+
+        def wt(shape, dtype, name, bufs):
+            t = work.tile(shape, dtype, name=name, tag=name, bufs=bufs, align_bytes=64)
+            return t
+
+        def bank_gw():
+            t = psum.tile([P, HALF], F32, name="gw_bank", tag="gw_bank", bufs=6)
+            return t
+
+        def bank_aux(shape, dtype):
+            t = psum.tile(shape, dtype, name="aux_bank", tag="aux_bank", bufs=2)
+            return t
+
+        xs = kt([P, NQ, 4], F32, "xs")
+        xb = [kt([P, 4, DI], U8, f"xb{q}") for q in range(NQ)]
+        gr = [[kt([P, 4, HALF], BF16, f"gr{q}_{h}") for h in range(NG)] for q in range(NQ)]
+        vr = [[kt([P, 4, HALF], BF16, f"vr{s}_{h}") for h in range(NG)] for s in range(2)]
+        vt = [[kt([P, DI], F32, f"vt{h}_{u}") for u in range(2)] for h in range(NG)]
+        xc = kt([P, NQ, DI], U32, "xc")
+        xcs = kt([P, NQ, DI], U8, "xcs")
+        gc = kt([P, NQ, DO], U32, "gc")
+        gcs = kt([P, NQ, DO], U8, "gcs")
+        dc = kt([P, NG, DI], U32, "dc")
+        dcs = kt([P, NG, DI], U8, "dcs")
+        ww = kt([P, NG, 2 * R], U8, "ww")
+        ws = kt([P, NG, R], U8, "ws")
+        mt = kt([P, NG, 4], BF16, "mt")
+        n2 = kt([P, NG, 4], F32, "n2")
+        nrm = kt([P, NG, 4], F32, "nrm")
+        rn = kt([P, NG, 4], F32, "rn")
+        beta = kt([P, NG, 4], F32, "beta")
+        r2 = kt([P, NG, 4], F32, "r2")
+        negr = kt([P, NG, 4], F32, "negr")
+        gam = kt([P, NG, 4], F32, "gam")
+        idb = kt([P, P], BF16, "idb")
+        idf = kt([P, P], F32, "idf")
+        warm = kt([P, 1], F32, "warm")
+
+        g4 = g.rearrange("(q p j) o -> q p j o", p=P, j=4)
+        x4 = x_bytes.rearrange("(q p j) i -> q p j i", p=P, j=4)
+        v4 = v.rearrange("(s n p) o -> s p n o", p=P, n=4)
+        nc.scalar.dma_start(out=xs[:], in_=x_scale.rearrange("(q p j) o -> p q (j o)", p=P, j=4))
+
+        def load_g(q, h):
+            nc.sync.dma_start(out=gr[q][h][:], in_=g4[q][:, :, HALF * h : HALF * (h + 1)])
+
+        def load_v(h):
+            for s in range(2):
+                nc.sync.dma_start(out=vr[s][h][:], in_=v4[s][:, :, HALF * h : HALF * (h + 1)])
+
+        nc.sync.dma_start(out=xb[0][:, 0:2, :], in_=x4[0][:, 0:2, :])
+        nc.sync.dma_start(out=xb[0][:, 2:4, :], in_=x4[0][:, 2:4, :])
+        load_g(0, 0)
+        nc.sync.dma_start(out=xb[1][:], in_=x4[1])
+        load_v(0)
+        nc.sync.dma_start(out=xb[2][:], in_=x4[2])
+        load_g(1, 0)
+        nc.sync.dma_start(out=xb[3][:], in_=x4[3])
+        load_g(2, 0)
+        load_v(1)
+        load_g(3, 0)
+        for q in range(NQ):
+            load_g(q, 1)
+        nc.gpsimd.memset(warm[:], 1.0)
+        make_identity(nc, idb[:])
+        make_identity(nc, idf[:])
+        nc.gpsimd.memset(ws[:].rearrange("p g n -> p (g n)").bitcast(I32), 0)
+        nc.sync.dma_start(out=mt[:], in_=m.rearrange("(h p t) -> p h t", p=P, t=4))
+        nc.sync.dma_start(out=ww[:].rearrange("p g n -> p (g n)").bitcast(I32).rearrange("p (g n) -> p g n", g=NG),
+                          in_=b_words.bitcast(I32).rearrange("g p n -> p g n"))
+        ws32 = ws[:].rearrange("p g n -> p (g n)").bitcast(I32).rearrange("p (g n) -> p g n", g=NG)
+        bs32 = b_scales.bitcast(I32)
+        for quad in range(4):
+            nc.sync.dma_start(out=ws32[32 * quad : 32 * quad + 4, :, :],
+                              in_=bs32[:, 4 * quad : 4 * quad + 4, :].rearrange("g q n -> q g n"))
+
+        nc.scalar.activation(warm[:], warm[:], ACT.Sqrt)
+
+        xp = {}
+        xi = {}
+        gi = {}
+
+        def widen_v(q, j):
+            nc.vector.tensor_scalar(out=xp[q][:, j, :], in0=xb[q][:, j, :].bitcast(FP8), scalar1=xs[:, q, j : j + 1], scalar2=None, op0=ALU.mult)
+
+        def widen_s(q, j):
+            nc.scalar.activation(xp[q][:, j, :], xb[q][:, j, :].bitcast(FP8), ACT.Copy, scale=xs[:, q, j : j + 1])
+
+        def new_xp(q):
+            xp[q] = wt([P, 4, DI], BF16, "xp", 2)
+
+        def ileave_x(q, h):
+            xi[q, h] = wt([P, 4 * HALF], BF16, "xi", 3)
+            nc.vector.tensor_copy(
+                out=xi[q, h][:].rearrange("p (c i t) -> p c t i", i=4, t=4),
+                in_=xp[q][:, :, HALF * h : HALF * (h + 1)].rearrange("p t (c i) -> p c t i", i=4),
+            )
+
+        def quant_x(q, h):
+            cols = slice(HALF * h, HALF * (h + 1))
+            nc.vector.quantize_mx(out=xc[:, q, cols].bitcast(E4M3X4), scales=xcs[:, q, cols], in_=xi[q, h][:])
+
+        def ileave_g(q, h):
+            gi[q, h] = wt([P, 4 * HALF], BF16, "gi", 3)
+            by_t = gr[q][h][:].rearrange("p j (m t) -> p t m j", t=4)
+            for s in range(2):
+                bank = bank_aux([P, 2 * HALF], BF16)
+                for e in range(2):
+                    nc.tensor.matmul(bank[:, HALF * e : HALF * (e + 1)], lhsT=idb[:], rhs=by_t[:, 2 * s + e], start=True, stop=True)
+                nc.scalar.copy(gi[q, h][:, 1024 * s : 1024 * (s + 1)], bank[:])
+
+        def ileave_g_v(q, h):
+            gi[q, h] = wt([P, 4 * HALF], BF16, "gi", 3)
+            nc.vector.tensor_copy(
+                out=gi[q, h][:].rearrange("p (t m j) -> p t m j", t=4, j=4),
+                in_=gr[q][h][:].rearrange("p j (m t) -> p t m j", t=4),
+            )
+
+        def quant_g(q, h):
+            cols = slice(HALF * h, HALF * (h + 1))
+            nc.vector.quantize_mx(out=gc[:, q, cols].bitcast(E4M3X4), scales=gcs[:, q, cols], in_=gi[q, h][:])
+
+        def vt_bf(h, t):
+            u, e = divmod(t, 2)
+            return vt[h][u][:].bitcast(BF16).rearrange("p (i e) -> p i e", e=2)[:, :, e]
+
+        def turn_v(h, u):
+            for s in range(2):
+                bank = bank_aux([P, HALF], F32)
+                for a in range(4):
+                    words = vr[s][h][:, a, :].bitcast(F32)
+                    nc.tensor.transpose(bank[:, P * a : P * (a + 1)], words[:, u : 256 : 2], idf[:])
+                nc.scalar.copy(vt[h][u][:, HALF * s : HALF * (s + 1)], bank[:])
+            for e in range(2):
+                t = 2 * u + e
+                dump = wt([P, DI], BF16, "sq_dump", 1)
+                nc.scalar.activation(dump[:], vt_bf(h, t), ACT.Square, accum_out=n2[:, h, t : t + 1])
+
+        def root(h):
+            nc.scalar.activation(nrm[:, h, :], n2[:, h, :], ACT.Sqrt)
+
+        def factors(h):
+            nc.vector.reciprocal(r2[:, h, :], n2[:, h, :])
+            nc.vector.reciprocal(rn[:, h, :], nrm[:, h, :])
+            nc.gpsimd.tensor_scalar(negr[:, h, :], r2[:, h, :], -1.0, None, op0=ALU.mult)
+            nc.gpsimd.tensor_tensor(beta[:, h, :], rn[:, h, :], mt[:, h, :], op=ALU.mult)
+
+        banks = {}
+
+        def mm1(k, q):
+            for h in range(2):
+                if q == 0:
+                    banks[k, h] = bank_gw()
+                nc.tensor.matmul_mx(
+                    banks[k, h][:],
+                    lhsT=gc[:, q, P * k : P * (k + 1)].bitcast(E4M3X4), lhsT_scale=gcs[:, q, P * k : P * (k + 1)],
+                    rhs=xc[:, q, HALF * h : HALF * (h + 1)].bitcast(E4M3X4), rhs_scale=xcs[:, q, HALF * h : HALF * (h + 1)],
+                    start=(q == 0), stop=(q == NQ - 1),
+                )
+
+        gw = {}
+        dvp = {}
+        dvi = {}
+
+        def evac(k):
+            h, t = divmod(k, 4)
+            gw[k] = wt([P, DI], F32, "gw", 4)
+            for s in range(2):
+                nc.scalar.activation(gw[k][:, HALF * s : HALF * (s + 1)], banks[k, s][:], ACT.Copy, scale=beta[:, h, t : t + 1])
+
+        def fold(k):
+            h, t = divmod(k, 4)
+            dump = wt([P, DI], F32, "fold_dump", 1)
+            nc.vector.scalar_tensor_tensor(out=dump[:], in0=gw[k][:], scalar=negr[:, h, t : t + 1], in1=vt_bf(h, t), op0=ALU.mult, op1=ALU.mult, accum_out=gam[:, h, t : t + 1])
+
+        def direction(k, cols=slice(0, DI)):
+            h, t = divmod(k, 4)
+            if t == 0:
+                dvp[h] = wt([P, 4, DI], BF16, "dvp", 2)
+            nc.vector.scalar_tensor_tensor(out=dvp[h][:, t, cols], in0=vt_bf(h, t)[:, cols], scalar=gam[:, h, t : t + 1], in1=gw[k][:, cols], op0=ALU.mult, op1=ALU.add)
+
+        def ileave_d(h, c, copy):
+            dvi[h, c] = wt([P, 1024], BF16, "dvi", 4)
+            copy(
+                dvi[h, c][:].rearrange("p (c i t) -> p c t i", i=4, t=4),
+                dvp[h][:, :, 256 * c : 256 * (c + 1)].rearrange("p t (c i) -> p c t i", i=4),
+            )
+
+        def quant_d(h, c):
+            cols = slice(256 * c, 256 * (c + 1))
+            nc.vector.quantize_mx(out=dc[:, h, cols].bitcast(E4M3X4), scales=dcs[:, h, cols], in_=dvi[h, c][:])
+
+        def mm2(c):
+            bank = bank_aux([P, 2, R], F32)
+            for a in range(2):
+                rows = slice(256 * c + P * a, 256 * c + P * (a + 1))
+                for r0 in range(0, R, P):
+                    for h in range(NG):
+                        nc.tensor.matmul_mx(
+                            bank[:, a, r0 : r0 + P],
+                            lhsT=dc[:, h, rows].bitcast(E4M3X4), lhsT_scale=dcs[:, h, rows],
+                            rhs=ww[:, h, 2 * r0 : 2 * (r0 + P)].bitcast(E2M1X4), rhs_scale=ws[:, h, r0 : r0 + P],
+                            start=(h == 0), stop=(h == NG - 1),
+                        )
+            res = wt([P, 2, R], F32, "res", 3)
+            nc.scalar.copy(res[:], bank[:])
+            nc.sync.dma_start(out=out[256 * c : 256 * (c + 1), :].rearrange("(a p) r -> p a r", p=P), in_=res[:])
+
+        v_list = {q: [j for j in range(4) if j not in SCALAR_WIDENS[q]] for q in range(NQ)}
+
+        def widens_s(q):
+            for j in SCALAR_WIDENS[q]:
+                widen_s(q, j)
+
+        def step_v(q):
+            ileave_x(q, 0)
+            ileave_x(q, 1)
+            vl = v_list[q + 1] if q + 1 < NQ else []
+            for j in vl[:1]:
+                widen_v(q + 1, j)
+            if q == 3:
+                ileave_g_v(3, 1)
+            quant_x(q, 0)
+            for j in vl[1:]:
+                widen_v(q + 1, j)
+            quant_x(q, 1)
+
+        new_xp(0)
+        new_xp(1)
+        for j in v_list[0]:
+            widen_v(0, j)
+        widens_s(0)
+        ileave_g(0, 0)
+        widens_s(1)
+        step_v(0)
+        quant_g(0, 0)
+        turn_v(0, 0)
+        for k in range(3):
+            mm1(k, 0)
+        new_xp(2)
+        widens_s(2)
+        ileave_g(1, 0)
+        step_v(1)
+        quant_g(1, 0)
+        turn_v(0, 1)
+        root(0)
+        for k in range(3):
+            mm1(k, 1)
+        new_xp(3)
+        widens_s(3)
+        ileave_g(2, 0)
+        step_v(2)
+        ileave_g(3, 0)
+        turn_v(1, 0)
+        ileave_g(0, 1)
+        ileave_x(3, 0)
+        ileave_x(3, 1)
+        quant_g(2, 0)
+        factors(0)
+        for k in range(3):
+            mm1(k, 2)
+        quant_x(3, 0)
+        quant_g(3, 0)
+        quant_x(3, 1)
+        for k in range(3):
+            mm1(k, 3)
+        ileave_g_v(3, 1)
+        evac(0)
+        evac(1)
+        ileave_g(1, 1)
+        quant_g(3, 1)
+        for q in range(NQ):
+            mm1(3, q)
+        fold(0)
+        quant_g(0, 1)
+        evac(2)
+        ileave_g(2, 1)
+        fold(1)
+        direction(0)
+        quant_g(1, 1)
+        fold(2)
+        quant_g(2, 1)
+        direction(1)
+        evac(3)
+        turn_v(1, 1)
+        fold(3)
+        direction(2)
+        for k in (4, 5, 6):
+            for q in range(NQ):
+                mm1(k, q)
+        root(1)
+        factors(1)
+        direction(3)
+        evac(4)
+        evac(5)
+        fold(4)
+        for q in range(NQ):
+            mm1(7, q)
+        ileave_d(0, 0, nc.scalar.copy)
+        evac(6)
+        fold(5)
+        direction(4)
+        ileave_d(0, 1, nc.scalar.copy)
+        evac(7)
+        fold(6)
+        direction(5)
+        quant_d(0, 0)
+        ileave_d(0, 2, nc.scalar.copy)
+        fold(7)
+        direction(6)
+        quant_d(0, 1)
+        ileave_d(0, 3, nc.scalar.copy)
+        direction(7, slice(0, HALF))
+        quant_d(0, 2)
+        ileave_d(1, 0, nc.vector.tensor_copy)
+        ileave_d(1, 1, nc.scalar.copy)
+        direction(7, slice(HALF, DI))
+        quant_d(0, 3)
+        quant_d(1, 0)
+        ileave_d(1, 2, nc.vector.tensor_copy)
+        ileave_d(1, 3, nc.scalar.copy)
+        mm2(0)
+        quant_d(1, 1)
+        mm2(1)
+        quant_d(1, 2)
+        mm2(2)
+        quant_d(1, 3)
+        mm2(3)

@@ -22,7 +22,7 @@ NQ = T // 512
 NG = DO // 512
 HALF = 512
 
-SCALAR_WIDENS = {0: (3,), 1: (2, 3), 2: (2, 3), 3: (2, 3)}
+SCALAR_WIDENS = {0: (3,), 1: (), 2: (), 3: ()}
 
 
 def tile_doradirectiongradienttoloradown_w4_kernel(tc, x_bytes, x_scale, g, v, m, b_words, b_scales, out):
@@ -70,7 +70,6 @@ def tile_doradirectiongradienttoloradown_w4_kernel(tc, x_bytes, x_scale, g, v, m
         r2 = kt([P, NG, 4], F32, "r2")
         negr = kt([P, NG, 4], F32, "negr")
         gam = kt([P, NG, 4], F32, "gam")
-        idb = kt([P, P], BF16, "idb")
         idf = kt([P, P], F32, "idf")
         warm = kt([P, 1], F32, "warm")
 
@@ -100,7 +99,6 @@ def tile_doradirectiongradienttoloradown_w4_kernel(tc, x_bytes, x_scale, g, v, m
         for q in range(NQ):
             load_g(q, 1)
         nc.gpsimd.memset(warm[:], 1.0)
-        make_identity(nc, idb[:])
         make_identity(nc, idf[:])
         nc.gpsimd.memset(ws[:].rearrange("p g n -> p (g n)").bitcast(I32), 0)
         nc.sync.dma_start(out=mt[:], in_=m.rearrange("(h p t) -> p h t", p=P, t=4))
@@ -138,20 +136,11 @@ def tile_doradirectiongradienttoloradown_w4_kernel(tc, x_bytes, x_scale, g, v, m
             cols = slice(HALF * h, HALF * (h + 1))
             nc.vector.quantize_mx(out=xc[:, q, cols].bitcast(E4M3X4), scales=xcs[:, q, cols], in_=xi[q, h][:])
 
-        def ileave_g(q, h):
+        def ileave_g(q, h, copy=nc.scalar.copy):
             gi[q, h] = wt([P, 4 * HALF], BF16, "gi", 3)
-            by_t = gr[q][h][:].rearrange("p j (m t) -> p t m j", t=4)
-            for s in range(2):
-                bank = bank_aux([P, 2 * HALF], BF16)
-                for e in range(2):
-                    nc.tensor.matmul(bank[:, HALF * e : HALF * (e + 1)], lhsT=idb[:], rhs=by_t[:, 2 * s + e], start=True, stop=True)
-                nc.scalar.copy(gi[q, h][:, 1024 * s : 1024 * (s + 1)], bank[:])
-
-        def ileave_g_v(q, h):
-            gi[q, h] = wt([P, 4 * HALF], BF16, "gi", 3)
-            nc.vector.tensor_copy(
-                out=gi[q, h][:].rearrange("p (t m j) -> p t m j", t=4, j=4),
-                in_=gr[q][h][:].rearrange("p j (m t) -> p t m j", t=4),
+            copy(
+                gi[q, h][:].rearrange("p (t m j) -> p t m j", t=4, j=4),
+                gr[q][h][:].rearrange("p j (m t) -> p t m j", t=4),
             )
 
         def quant_g(q, h):
@@ -254,12 +243,10 @@ def tile_doradirectiongradienttoloradown_w4_kernel(tc, x_bytes, x_scale, g, v, m
             ileave_x(q, 0)
             ileave_x(q, 1)
             vl = v_list[q + 1] if q + 1 < NQ else []
-            for j in vl[:1]:
+            for j in vl[:2]:
                 widen_v(q + 1, j)
-            if q == 3:
-                ileave_g_v(3, 1)
             quant_x(q, 0)
-            for j in vl[1:]:
+            for j in vl[2:]:
                 widen_v(q + 1, j)
             quant_x(q, 1)
 
@@ -279,9 +266,9 @@ def tile_doradirectiongradienttoloradown_w4_kernel(tc, x_bytes, x_scale, g, v, m
         widens_s(2)
         ileave_g(1, 0)
         step_v(1)
-        quant_g(1, 0)
         turn_v(0, 1)
         root(0)
+        quant_g(1, 0)
         for k in range(3):
             mm1(k, 1)
         new_xp(3)
@@ -290,11 +277,11 @@ def tile_doradirectiongradienttoloradown_w4_kernel(tc, x_bytes, x_scale, g, v, m
         step_v(2)
         ileave_g(3, 0)
         turn_v(1, 0)
+        quant_g(2, 0)
         ileave_g(0, 1)
         ileave_x(3, 0)
-        ileave_x(3, 1)
-        quant_g(2, 0)
         factors(0)
+        ileave_x(3, 1)
         for k in range(3):
             mm1(k, 2)
         quant_x(3, 0)
@@ -302,20 +289,20 @@ def tile_doradirectiongradienttoloradown_w4_kernel(tc, x_bytes, x_scale, g, v, m
         quant_x(3, 1)
         for k in range(3):
             mm1(k, 3)
-        ileave_g_v(3, 1)
+        ileave_g(3, 1, nc.vector.tensor_copy)
         evac(0)
         evac(1)
-        ileave_g(1, 1)
+        quant_g(0, 1)
         quant_g(3, 1)
         for q in range(NQ):
             mm1(3, q)
         fold(0)
-        quant_g(0, 1)
-        evac(2)
-        ileave_g(2, 1)
+        ileave_g(1, 1)
         fold(1)
+        evac(2)
         direction(0)
         quant_g(1, 1)
+        ileave_g(2, 1, nc.vector.tensor_copy)
         fold(2)
         quant_g(2, 1)
         direction(1)

@@ -22,7 +22,7 @@ NQ = T // 512
 NG = DO // 512
 HALF = 512
 
-SCALAR_WIDENS = {0: (3,), 1: (), 2: (), 3: ()}
+SCALAR_WIDENS = {0: (2, 3), 1: (0, 1, 2, 3), 2: (0, 1, 2, 3), 3: (0, 1, 2, 3)}
 
 
 def tile_doradirectiongradienttoloradown_w4_kernel(tc, x_bytes, x_scale, g, v, m, b_words, b_scales, out):
@@ -51,7 +51,7 @@ def tile_doradirectiongradienttoloradown_w4_kernel(tc, x_bytes, x_scale, g, v, m
 
         xs = kt([P, NQ, 4], F32, "xs")
         xb = [kt([P, 4, DI], U8, f"xb{q}") for q in range(NQ)]
-        gr = [[kt([P, 4, HALF], BF16, f"gr{q}_{h}") for h in range(NG)] for q in range(NQ)]
+        gr = [kt([P, 4, DO], BF16, f"gr{q}") for q in range(NQ)]
         vr = [[kt([P, 4, HALF], BF16, f"vr{s}_{h}") for h in range(NG)] for s in range(2)]
         vt = [[kt([P, DI], F32, f"vt{h}_{u}") for u in range(2)] for h in range(NG)]
         xc = kt([P, NQ, DI], U32, "xc")
@@ -78,8 +78,11 @@ def tile_doradirectiongradienttoloradown_w4_kernel(tc, x_bytes, x_scale, g, v, m
         v4 = v.rearrange("(s n p) o -> s p n o", p=P, n=4)
         nc.scalar.dma_start(out=xs[:], in_=x_scale.rearrange("(q p j) o -> p q (j o)", p=P, j=4))
 
-        def load_g(q, h):
-            nc.sync.dma_start(out=gr[q][h][:], in_=g4[q][:, :, HALF * h : HALF * (h + 1)])
+        def load_x(q):
+            nc.sync.dma_start(out=xb[q][:], in_=x4[q])
+
+        def load_g(q):
+            nc.sync.dma_start(out=gr[q][:], in_=g4[q])
 
         def load_v(h):
             for s in range(2):
@@ -87,17 +90,15 @@ def tile_doradirectiongradienttoloradown_w4_kernel(tc, x_bytes, x_scale, g, v, m
 
         nc.sync.dma_start(out=xb[0][:, 0:2, :], in_=x4[0][:, 0:2, :])
         nc.sync.dma_start(out=xb[0][:, 2:4, :], in_=x4[0][:, 2:4, :])
-        load_g(0, 0)
-        nc.sync.dma_start(out=xb[1][:], in_=x4[1])
+        load_x(1)
+        load_g(0)
         load_v(0)
-        nc.sync.dma_start(out=xb[2][:], in_=x4[2])
-        load_g(1, 0)
-        nc.sync.dma_start(out=xb[3][:], in_=x4[3])
-        load_g(2, 0)
+        load_x(2)
+        load_g(1)
+        load_x(3)
+        load_g(2)
         load_v(1)
-        load_g(3, 0)
-        for q in range(NQ):
-            load_g(q, 1)
+        load_g(3)
         nc.gpsimd.memset(warm[:], 1.0)
         make_identity(nc, idf[:])
         nc.gpsimd.memset(ws[:].rearrange("p g n -> p (g n)").bitcast(I32), 0)
@@ -140,7 +141,7 @@ def tile_doradirectiongradienttoloradown_w4_kernel(tc, x_bytes, x_scale, g, v, m
             gi[q, h] = wt([P, 4 * HALF], BF16, "gi", 3)
             copy(
                 gi[q, h][:].rearrange("p (t m j) -> p t m j", t=4, j=4),
-                gr[q][h][:].rearrange("p j (m t) -> p t m j", t=4),
+                gr[q][:, :, HALF * h : HALF * (h + 1)].rearrange("p j (m t) -> p t m j", t=4),
             )
 
         def quant_g(q, h):
@@ -233,88 +234,85 @@ def tile_doradirectiongradienttoloradown_w4_kernel(tc, x_bytes, x_scale, g, v, m
             nc.scalar.copy(res[:], bank[:])
             nc.sync.dma_start(out=out[256 * c : 256 * (c + 1), :].rearrange("(a p) r -> p a r", p=P), in_=res[:])
 
-        v_list = {q: [j for j in range(4) if j not in SCALAR_WIDENS[q]] for q in range(NQ)}
-
-        def widens_s(q):
-            for j in SCALAR_WIDENS[q]:
-                widen_s(q, j)
-
-        def step_v(q):
+        def ix(q):
             ileave_x(q, 0)
             ileave_x(q, 1)
-            vl = v_list[q + 1] if q + 1 < NQ else []
-            for j in vl[:2]:
-                widen_v(q + 1, j)
+
+        def qx(q):
             quant_x(q, 0)
-            for j in vl[2:]:
-                widen_v(q + 1, j)
             quant_x(q, 1)
 
-        new_xp(0)
-        new_xp(1)
-        for j in v_list[0]:
-            widen_v(0, j)
-        widens_s(0)
-        ileave_g(0, 0)
-        widens_s(1)
-        step_v(0)
+        def widen(q):
+            new_xp(q)
+            for j in range(4):
+                if j in SCALAR_WIDENS[q]:
+                    widen_s(q, j)
+                else:
+                    widen_v(q, j)
+
+        def mm_pass(q):
+            for k in range(3):
+                mm1(k, q)
+
+        widen(0)
+        widen(1)
+        ix(0)
+        ileave_g(0, 0, nc.vector.tensor_copy)
+        qx(0)
         quant_g(0, 0)
         turn_v(0, 0)
-        for k in range(3):
-            mm1(k, 0)
-        new_xp(2)
-        widens_s(2)
-        ileave_g(1, 0)
-        step_v(1)
+        mm_pass(0)
+        widen(2)
+        ileave_g(0, 1, nc.vector.tensor_copy)
+        ix(1)
+        quant_g(0, 1)
+        ileave_g(1, 0, nc.vector.tensor_copy)
+        qx(1)
+        quant_g(1, 0)
         turn_v(0, 1)
         root(0)
-        quant_g(1, 0)
-        for k in range(3):
-            mm1(k, 1)
-        new_xp(3)
-        widens_s(3)
-        ileave_g(2, 0)
-        step_v(2)
+        mm_pass(1)
+        widen(3)
+        ix(2)
+        factors(0)
+        ileave_g(1, 1, nc.vector.tensor_copy)
+        qx(2)
+        ileave_g(2, 0, nc.vector.tensor_copy)
+        quant_g(1, 1)
+        ileave_g(2, 1, nc.vector.tensor_copy)
+        quant_g(2, 0)
+        quant_g(2, 1)
         ileave_g(3, 0)
         turn_v(1, 0)
-        quant_g(2, 0)
-        ileave_g(0, 1)
-        ileave_x(3, 0)
-        factors(0)
-        ileave_x(3, 1)
-        for k in range(3):
-            mm1(k, 2)
-        quant_x(3, 0)
+        mm_pass(2)
+        ix(3)
         quant_g(3, 0)
-        quant_x(3, 1)
+        qx(3)
         for k in range(3):
             mm1(k, 3)
         ileave_g(3, 1, nc.vector.tensor_copy)
         evac(0)
         evac(1)
-        quant_g(0, 1)
         quant_g(3, 1)
         for q in range(NQ):
             mm1(3, q)
         fold(0)
-        ileave_g(1, 1)
-        fold(1)
         evac(2)
+        fold(1)
         direction(0)
-        quant_g(1, 1)
-        ileave_g(2, 1, nc.vector.tensor_copy)
-        fold(2)
-        quant_g(2, 1)
-        direction(1)
         evac(3)
         turn_v(1, 1)
+        root(1)
+        for q in range(NQ):
+            mm1(4, q)
+        fold(2)
+        direction(1)
         fold(3)
-        direction(2)
-        for k in (4, 5, 6):
+        factors(1)
+        for k in (5, 6):
             for q in range(NQ):
                 mm1(k, q)
-        root(1)
-        factors(1)
+        direction(2)
         direction(3)
         evac(4)
         evac(5)

@@ -22,7 +22,7 @@ NQ = T // 512
 NG = DO // 512
 HALF = 512
 
-SCALAR_WIDENS = {0: (2, 3), 1: (0, 1, 2, 3), 2: (0, 1, 2, 3), 3: (0, 1, 2, 3)}
+SCALAR_WIDENS = {0: (0, 2, 3), 1: (0, 1, 2, 3), 2: (0, 1, 2, 3), 3: (0, 1, 2, 3)}
 
 
 def tile_doradirectiongradienttoloradown_w4_kernel(tc, x_bytes, x_scale, g, v, m, b_words, b_scales, out):
@@ -88,16 +88,16 @@ def tile_doradirectiongradienttoloradown_w4_kernel(tc, x_bytes, x_scale, g, v, m
             for s in range(2):
                 nc.sync.dma_start(out=vr[s][h][:], in_=v4[s][:, :, HALF * h : HALF * (h + 1)])
 
-        nc.sync.dma_start(out=xb[0][:, 0:2, :], in_=x4[0][:, 0:2, :])
-        nc.sync.dma_start(out=xb[0][:, 2:4, :], in_=x4[0][:, 2:4, :])
+        for h in range(NG):
+            nc.sync.dma_start(out=xb[0][:, 2 * h : 2 * h + 2, :], in_=x4[0][:, 2 * h : 2 * h + 2, :])
+            nc.sync.dma_start(out=gr[0][:, :, HALF * h : HALF * (h + 1)], in_=g4[0][:, :, HALF * h : HALF * (h + 1)])
         load_x(1)
-        load_g(0)
         load_v(0)
         load_x(2)
         load_g(1)
         load_x(3)
-        load_g(2)
         load_v(1)
+        load_g(2)
         load_g(3)
         nc.gpsimd.memset(warm[:], 1.0)
         make_identity(nc, idf[:])
@@ -126,16 +126,15 @@ def tile_doradirectiongradienttoloradown_w4_kernel(tc, x_bytes, x_scale, g, v, m
         def new_xp(q):
             xp[q] = wt([P, 4, DI], BF16, "xp", 2)
 
-        def ileave_x(q, h):
-            xi[q, h] = wt([P, 4 * HALF], BF16, "xi", 3)
+        def ileave_x(q):
+            xi[q] = wt([P, 4 * DI], BF16, "xi", 2)
             nc.vector.tensor_copy(
-                out=xi[q, h][:].rearrange("p (c i t) -> p c t i", i=4, t=4),
-                in_=xp[q][:, :, HALF * h : HALF * (h + 1)].rearrange("p t (c i) -> p c t i", i=4),
+                out=xi[q][:].rearrange("p (c i t) -> p c t i", i=4, t=4),
+                in_=xp[q][:].rearrange("p t (c i) -> p c t i", i=4),
             )
 
-        def quant_x(q, h):
-            cols = slice(HALF * h, HALF * (h + 1))
-            nc.vector.quantize_mx(out=xc[:, q, cols].bitcast(E4M3X4), scales=xcs[:, q, cols], in_=xi[q, h][:])
+        def quant_x(q):
+            nc.vector.quantize_mx(out=xc[:, q, :].bitcast(E4M3X4), scales=xcs[:, q, :], in_=xi[q][:])
 
         def ileave_g(q, h, copy=nc.scalar.copy):
             gi[q, h] = wt([P, 4 * HALF], BF16, "gi", 3)
@@ -159,10 +158,19 @@ def tile_doradirectiongradienttoloradown_w4_kernel(tc, x_bytes, x_scale, g, v, m
                     words = vr[s][h][:, a, :].bitcast(F32)
                     nc.tensor.transpose(bank[:, P * a : P * (a + 1)], words[:, u : 256 : 2], idf[:])
                 nc.scalar.copy(vt[h][u][:, HALF * s : HALF * (s + 1)], bank[:])
-            for e in range(2):
-                t = 2 * u + e
-                dump = wt([P, DI], BF16, "sq_dump", 1)
-                nc.scalar.activation(dump[:], vt_bf(h, t), ACT.Square, accum_out=n2[:, h, t : t + 1])
+
+        def gram(h):
+            bank = bank_aux([P, 4, P], F32)
+            for t in range(4):
+                for n in range(8):
+                    cols = vr[n // 4][h][:, n % 4, t : HALF : 4]
+                    nc.tensor.matmul(bank[:, t, :], lhsT=cols, rhs=cols, start=(n == 0), stop=(n == 7))
+            return bank
+
+        def norms(h, bank):
+            for t in range(4):
+                dump = wt([P, P], F32, "norm_dump", 2)
+                nc.vector.scalar_tensor_tensor(out=dump[:], in0=bank[:, t, :], scalar=1.0, in1=idf[:], op0=ALU.mult, op1=ALU.mult, accum_out=n2[:, h, t : t + 1])
 
         def root(h):
             nc.scalar.activation(nrm[:, h, :], n2[:, h, :], ACT.Sqrt)
@@ -218,29 +226,22 @@ def tile_doradirectiongradienttoloradown_w4_kernel(tc, x_bytes, x_scale, g, v, m
             cols = slice(256 * c, 256 * (c + 1))
             nc.vector.quantize_mx(out=dc[:, h, cols].bitcast(E4M3X4), scales=dcs[:, h, cols], in_=dvi[h, c][:])
 
-        def mm2(c):
-            bank = bank_aux([P, 2, R], F32)
+        def mm2(c, copies):
+            rows_out = out[256 * c : 256 * (c + 1), :].rearrange("(a p) r -> a p r", p=P)
             for a in range(2):
+                bank = bank_gw()
                 rows = slice(256 * c + P * a, 256 * c + P * (a + 1))
                 for r0 in range(0, R, P):
                     for h in range(NG):
                         nc.tensor.matmul_mx(
-                            bank[:, a, r0 : r0 + P],
+                            bank[:, r0 : r0 + P],
                             lhsT=dc[:, h, rows].bitcast(E4M3X4), lhsT_scale=dcs[:, h, rows],
                             rhs=ww[:, h, 2 * r0 : 2 * (r0 + P)].bitcast(E2M1X4), rhs_scale=ws[:, h, r0 : r0 + P],
                             start=(h == 0), stop=(h == NG - 1),
                         )
-            res = wt([P, 2, R], F32, "res", 3)
-            nc.scalar.copy(res[:], bank[:])
-            nc.sync.dma_start(out=out[256 * c : 256 * (c + 1), :].rearrange("(a p) r -> p a r", p=P), in_=res[:])
-
-        def ix(q):
-            ileave_x(q, 0)
-            ileave_x(q, 1)
-
-        def qx(q):
-            quant_x(q, 0)
-            quant_x(q, 1)
+                res = wt([P, R], F32, "res", 4)
+                copies[a](res[:], bank[:, 0:R])
+                nc.sync.dma_start(out=rows_out[a], in_=res[:])
 
         def widen(q):
             new_xp(q)
@@ -255,64 +256,67 @@ def tile_doradirectiongradienttoloradown_w4_kernel(tc, x_bytes, x_scale, g, v, m
                 mm1(k, q)
 
         widen(0)
-        widen(1)
-        ix(0)
         ileave_g(0, 0, nc.vector.tensor_copy)
-        qx(0)
         quant_g(0, 0)
-        turn_v(0, 0)
-        mm_pass(0)
-        widen(2)
         ileave_g(0, 1, nc.vector.tensor_copy)
-        ix(1)
+        widen(1)
+        ileave_x(0)
         quant_g(0, 1)
+        quant_x(0)
+        gram0 = gram(0)
+        mm_pass(0)
+        ileave_x(1)
+        widen(2)
+        turn_v(0, 0)
         ileave_g(1, 0, nc.vector.tensor_copy)
-        qx(1)
+        quant_x(1)
+        norms(0, gram0)
         quant_g(1, 0)
-        turn_v(0, 1)
         root(0)
         mm_pass(1)
+        ileave_g(1, 1)
+        ileave_x(2)
         widen(3)
-        ix(2)
         factors(0)
-        ileave_g(1, 1, nc.vector.tensor_copy)
-        qx(2)
-        ileave_g(2, 0, nc.vector.tensor_copy)
+        gram1 = gram(1)
         quant_g(1, 1)
-        ileave_g(2, 1, nc.vector.tensor_copy)
+        ileave_g(2, 0, nc.vector.tensor_copy)
+        quant_x(2)
         quant_g(2, 0)
-        quant_g(2, 1)
-        ileave_g(3, 0)
-        turn_v(1, 0)
+        norms(1, gram1)
         mm_pass(2)
-        ix(3)
+        ileave_g(3, 0)
+        root(1)
+        turn_v(0, 1)
+        ileave_x(3)
+        factors(1)
         quant_g(3, 0)
-        qx(3)
-        for k in range(3):
-            mm1(k, 3)
+        quant_x(3)
+        mm_pass(3)
+        ileave_g(2, 1)
         ileave_g(3, 1, nc.vector.tensor_copy)
+        quant_g(2, 1)
+        quant_g(3, 1)
         evac(0)
         evac(1)
-        quant_g(3, 1)
         for q in range(NQ):
             mm1(3, q)
         fold(0)
         evac(2)
+        turn_v(1, 0)
         fold(1)
         direction(0)
-        evac(3)
-        turn_v(1, 1)
-        root(1)
         for q in range(NQ):
             mm1(4, q)
         fold(2)
         direction(1)
+        evac(3)
+        turn_v(1, 1)
         fold(3)
-        factors(1)
+        direction(2)
         for k in (5, 6):
             for q in range(NQ):
                 mm1(k, q)
-        direction(2)
         direction(3)
         evac(4)
         evac(5)
@@ -342,10 +346,10 @@ def tile_doradirectiongradienttoloradown_w4_kernel(tc, x_bytes, x_scale, g, v, m
         quant_d(1, 0)
         ileave_d(1, 2, nc.vector.tensor_copy)
         ileave_d(1, 3, nc.scalar.copy)
-        mm2(0)
+        mm2(0, [nc.scalar.copy] * 2)
         quant_d(1, 1)
-        mm2(1)
+        mm2(1, [nc.scalar.copy] * 2)
         quant_d(1, 2)
-        mm2(2)
+        mm2(2, [nc.scalar.copy] * 2)
         quant_d(1, 3)
-        mm2(3)
+        mm2(3, [nc.scalar.copy, nc.vector.tensor_copy])

from contextlib import ExitStack

import concourse.mybir as mybir
from concourse.masks import make_identity

T, DI, DO, R = 2048, 1024, 1024, 256
FLOPS = 2 * T * DI * DO + 2 * DI * DO * R

P = 128
F32 = mybir.dt.float32
BF16 = mybir.dt.bfloat16
I32 = mybir.dt.int32
U32 = mybir.dt.uint32
U8 = mybir.dt.uint8
FP8 = mybir.dt.float8_e4m3fn
E4M3X4 = mybir.dt.float8_e4m3fn_x4
E2M1X4 = mybir.dt.float4_e2m1fn_x4
ACT = mybir.ActivationFunctionType
ALU = mybir.AluOpType

NQ = T // 512
NG = DO // 512
HALF = 512

SCALAR_WIDENS = {0: (0, 2, 3), 1: (0, 1, 2, 3), 2: (0, 1, 2, 3), 3: (0, 1, 2, 3)}


def tile_doradirectiongradienttoloradown_w4_kernel(tc, x_bytes, x_scale, g, v, m, b_words, b_scales, out):
    nc = tc.nc
    with ExitStack() as ctx:
        keep = ctx.enter_context(tc.tile_pool(name="keep", bufs=1))
        work = ctx.enter_context(tc.tile_pool(name="work", bufs=2))
        psum = ctx.enter_context(tc.psum_pool(name="psum", bufs=1))
        ctx.enter_context(tc.manual_schedule())

        def kt(shape, dtype, name):
            t = keep.tile(shape, dtype, name=name, align_bytes=64)
            return t

        def wt(shape, dtype, name, bufs):
            t = work.tile(shape, dtype, name=name, tag=name, bufs=bufs, align_bytes=64)
            return t

        def bank_gw():
            t = psum.tile([P, HALF], F32, name="gw_bank", tag="gw_bank", bufs=6)
            return t

        def bank_aux(shape, dtype):
            t = psum.tile(shape, dtype, name="aux_bank", tag="aux_bank", bufs=2)
            return t

        xs = kt([P, NQ, 4], F32, "xs")
        xb = [kt([P, 4, DI], U8, f"xb{q}") for q in range(NQ)]
        gr = [kt([P, 4, DO], BF16, f"gr{q}") for q in range(NQ)]
        vr = [[kt([P, 4, HALF], BF16, f"vr{s}_{h}") for h in range(NG)] for s in range(2)]
        vt = [[kt([P, DI], F32, f"vt{h}_{u}") for u in range(2)] for h in range(NG)]
        xc = kt([P, NQ, DI], U32, "xc")
        xcs = kt([P, NQ, DI], U8, "xcs")
        gc = kt([P, NQ, DO], U32, "gc")
        gcs = kt([P, NQ, DO], U8, "gcs")
        dc = kt([P, NG, DI], U32, "dc")
        dcs = kt([P, NG, DI], U8, "dcs")
        ww = kt([P, NG, 2 * R], U8, "ww")
        ws = kt([P, NG, R], U8, "ws")
        mt = kt([P, NG, 4], BF16, "mt")
        n2 = kt([P, NG, 4], F32, "n2")
        nrm = kt([P, NG, 4], F32, "nrm")
        rn = kt([P, NG, 4], F32, "rn")
        beta = kt([P, NG, 4], F32, "beta")
        r2 = kt([P, NG, 4], F32, "r2")
        negr = kt([P, NG, 4], F32, "negr")
        gam = kt([P, NG, 4], F32, "gam")
        idf = kt([P, P], F32, "idf")
        warm = kt([P, 1], F32, "warm")

        g4 = g.rearrange("(q p j) o -> q p j o", p=P, j=4)
        x4 = x_bytes.rearrange("(q p j) i -> q p j i", p=P, j=4)
        v4 = v.rearrange("(s n p) o -> s p n o", p=P, n=4)
        nc.scalar.dma_start(out=xs[:], in_=x_scale.rearrange("(q p j) o -> p q (j o)", p=P, j=4))

        def load_x(q):
            nc.sync.dma_start(out=xb[q][:], in_=x4[q])

        def load_g(q):
            nc.sync.dma_start(out=gr[q][:], in_=g4[q])

        def load_v(h):
            for s in range(2):
                nc.sync.dma_start(out=vr[s][h][:], in_=v4[s][:, :, HALF * h : HALF * (h + 1)])

        for h in range(NG):
            nc.sync.dma_start(out=xb[0][:, 2 * h : 2 * h + 2, :], in_=x4[0][:, 2 * h : 2 * h + 2, :])
            nc.sync.dma_start(out=gr[0][:, :, HALF * h : HALF * (h + 1)], in_=g4[0][:, :, HALF * h : HALF * (h + 1)])
        load_x(1)
        load_v(0)
        load_x(2)
        load_g(1)
        load_x(3)
        load_v(1)
        load_g(2)
        load_g(3)
        nc.gpsimd.memset(warm[:], 1.0)
        make_identity(nc, idf[:])
        nc.gpsimd.memset(ws[:].rearrange("p g n -> p (g n)").bitcast(I32), 0)
        nc.sync.dma_start(out=mt[:], in_=m.rearrange("(h p t) -> p h t", p=P, t=4))
        nc.sync.dma_start(out=ww[:].rearrange("p g n -> p (g n)").bitcast(I32).rearrange("p (g n) -> p g n", g=NG),
                          in_=b_words.bitcast(I32).rearrange("g p n -> p g n"))
        ws32 = ws[:].rearrange("p g n -> p (g n)").bitcast(I32).rearrange("p (g n) -> p g n", g=NG)
        bs32 = b_scales.bitcast(I32)
        for quad in range(4):
            nc.sync.dma_start(out=ws32[32 * quad : 32 * quad + 4, :, :],
                              in_=bs32[:, 4 * quad : 4 * quad + 4, :].rearrange("g q n -> q g n"))

        nc.scalar.activation(warm[:], warm[:], ACT.Sqrt)

        xp = {}
        xi = {}
        gi = {}

        def widen_v(q, j):
            nc.vector.tensor_scalar(out=xp[q][:, j, :], in0=xb[q][:, j, :].bitcast(FP8), scalar1=xs[:, q, j : j + 1], scalar2=None, op0=ALU.mult)

        def widen_s(q, j):
            nc.scalar.activation(xp[q][:, j, :], xb[q][:, j, :].bitcast(FP8), ACT.Copy, scale=xs[:, q, j : j + 1])

        def new_xp(q):
            xp[q] = wt([P, 4, DI], BF16, "xp", 2)

        def ileave_x(q):
            xi[q] = wt([P, 4 * DI], BF16, "xi", 2)
            nc.vector.tensor_copy(
                out=xi[q][:].rearrange("p (c i t) -> p c t i", i=4, t=4),
                in_=xp[q][:].rearrange("p t (c i) -> p c t i", i=4),
            )

        def quant_x(q):
            nc.vector.quantize_mx(out=xc[:, q, :].bitcast(E4M3X4), scales=xcs[:, q, :], in_=xi[q][:])

        def ileave_g(q, h, copy=nc.scalar.copy):
            gi[q, h] = wt([P, 4 * HALF], BF16, "gi", 3)
            copy(
                gi[q, h][:].rearrange("p (t m j) -> p t m j", t=4, j=4),
                gr[q][:, :, HALF * h : HALF * (h + 1)].rearrange("p j (m t) -> p t m j", t=4),
            )

        def quant_g(q, h):
            cols = slice(HALF * h, HALF * (h + 1))
            nc.vector.quantize_mx(out=gc[:, q, cols].bitcast(E4M3X4), scales=gcs[:, q, cols], in_=gi[q, h][:])

        def vt_bf(h, t):
            u, e = divmod(t, 2)
            return vt[h][u][:].bitcast(BF16).rearrange("p (i e) -> p i e", e=2)[:, :, e]

        def turn_v(h, u):
            for s in range(2):
                bank = bank_aux([P, HALF], F32)
                for a in range(4):
                    words = vr[s][h][:, a, :].bitcast(F32)
                    nc.tensor.transpose(bank[:, P * a : P * (a + 1)], words[:, u : 256 : 2], idf[:])
                nc.scalar.copy(vt[h][u][:, HALF * s : HALF * (s + 1)], bank[:])

        def gram(h):
            bank = bank_aux([P, 4, P], F32)
            for t in range(4):
                for n in range(8):
                    cols = vr[n // 4][h][:, n % 4, t : HALF : 4]
                    nc.tensor.matmul(bank[:, t, :], lhsT=cols, rhs=cols, start=(n == 0), stop=(n == 7))
            return bank

        def norms(h, bank):
            for t in range(4):
                dump = wt([P, P], F32, "norm_dump", 2)
                nc.vector.scalar_tensor_tensor(out=dump[:], in0=bank[:, t, :], scalar=1.0, in1=idf[:], op0=ALU.mult, op1=ALU.mult, accum_out=n2[:, h, t : t + 1])

        def root(h):
            nc.scalar.activation(nrm[:, h, :], n2[:, h, :], ACT.Sqrt)

        def factors(h):
            nc.vector.reciprocal(r2[:, h, :], n2[:, h, :])
            nc.vector.reciprocal(rn[:, h, :], nrm[:, h, :])
            nc.gpsimd.tensor_scalar(negr[:, h, :], r2[:, h, :], -1.0, None, op0=ALU.mult)
            nc.gpsimd.tensor_tensor(beta[:, h, :], rn[:, h, :], mt[:, h, :], op=ALU.mult)

        banks = {}

        def mm1(k, q):
            for h in range(2):
                if q == 0:
                    banks[k, h] = bank_gw()
                nc.tensor.matmul_mx(
                    banks[k, h][:],
                    lhsT=gc[:, q, P * k : P * (k + 1)].bitcast(E4M3X4), lhsT_scale=gcs[:, q, P * k : P * (k + 1)],
                    rhs=xc[:, q, HALF * h : HALF * (h + 1)].bitcast(E4M3X4), rhs_scale=xcs[:, q, HALF * h : HALF * (h + 1)],
                    start=(q == 0), stop=(q == NQ - 1),
                )

        gw = {}
        dvp = {}
        dvi = {}

        def evac(k):
            h, t = divmod(k, 4)
            gw[k] = wt([P, DI], F32, "gw", 4)
            for s in range(2):
                nc.scalar.activation(gw[k][:, HALF * s : HALF * (s + 1)], banks[k, s][:], ACT.Copy, scale=beta[:, h, t : t + 1])

        def fold(k):
            h, t = divmod(k, 4)
            dump = wt([P, DI], F32, "fold_dump", 1)
            nc.vector.scalar_tensor_tensor(out=dump[:], in0=gw[k][:], scalar=negr[:, h, t : t + 1], in1=vt_bf(h, t), op0=ALU.mult, op1=ALU.mult, accum_out=gam[:, h, t : t + 1])

        def direction(k, cols=slice(0, DI)):
            h, t = divmod(k, 4)
            if t == 0:
                dvp[h] = wt([P, 4, DI], BF16, "dvp", 2)
            nc.vector.scalar_tensor_tensor(out=dvp[h][:, t, cols], in0=vt_bf(h, t)[:, cols], scalar=gam[:, h, t : t + 1], in1=gw[k][:, cols], op0=ALU.mult, op1=ALU.add)

        def ileave_d(h, c, copy):
            dvi[h, c] = wt([P, 1024], BF16, "dvi", 4)
            copy(
                dvi[h, c][:].rearrange("p (c i t) -> p c t i", i=4, t=4),
                dvp[h][:, :, 256 * c : 256 * (c + 1)].rearrange("p t (c i) -> p c t i", i=4),
            )

        def quant_d(h, c):
            cols = slice(256 * c, 256 * (c + 1))
            nc.vector.quantize_mx(out=dc[:, h, cols].bitcast(E4M3X4), scales=dcs[:, h, cols], in_=dvi[h, c][:])

        def mm2(c, copies):
            rows_out = out[256 * c : 256 * (c + 1), :].rearrange("(a p) r -> a p r", p=P)
            for a in range(2):
                bank = bank_gw()
                rows = slice(256 * c + P * a, 256 * c + P * (a + 1))
                for r0 in range(0, R, P):
                    for h in range(NG):
                        nc.tensor.matmul_mx(
                            bank[:, r0 : r0 + P],
                            lhsT=dc[:, h, rows].bitcast(E4M3X4), lhsT_scale=dcs[:, h, rows],
                            rhs=ww[:, h, 2 * r0 : 2 * (r0 + P)].bitcast(E2M1X4), rhs_scale=ws[:, h, r0 : r0 + P],
                            start=(h == 0), stop=(h == NG - 1),
                        )
                res = wt([P, R], F32, "res", 4)
                copies[a](res[:], bank[:, 0:R])
                nc.sync.dma_start(out=rows_out[a], in_=res[:])

        def widen(q):
            new_xp(q)
            for j in range(4):
                if j in SCALAR_WIDENS[q]:
                    widen_s(q, j)
                else:
                    widen_v(q, j)

        def mm_pass(q):
            for k in range(3):
                mm1(k, q)

        widen(0)
        ileave_g(0, 0, nc.vector.tensor_copy)
        quant_g(0, 0)
        ileave_g(0, 1, nc.vector.tensor_copy)
        widen(1)
        ileave_x(0)
        quant_g(0, 1)
        quant_x(0)
        gram0 = gram(0)
        mm_pass(0)
        ileave_x(1)
        widen(2)
        turn_v(0, 0)
        ileave_g(1, 0, nc.vector.tensor_copy)
        quant_x(1)
        norms(0, gram0)
        quant_g(1, 0)
        root(0)
        mm_pass(1)
        ileave_g(1, 1)
        ileave_x(2)
        widen(3)
        factors(0)
        gram1 = gram(1)
        quant_g(1, 1)
        ileave_g(2, 0, nc.vector.tensor_copy)
        quant_x(2)
        quant_g(2, 0)
        norms(1, gram1)
        mm_pass(2)
        ileave_g(3, 0)
        root(1)
        turn_v(0, 1)
        ileave_x(3)
        factors(1)
        quant_g(3, 0)
        quant_x(3)
        mm_pass(3)
        ileave_g(2, 1)
        ileave_g(3, 1, nc.vector.tensor_copy)
        quant_g(2, 1)
        quant_g(3, 1)
        evac(0)
        evac(1)
        for q in range(NQ):
            mm1(3, q)
        fold(0)
        evac(2)
        turn_v(1, 0)
        fold(1)
        direction(0)
        for q in range(NQ):
            mm1(4, q)
        fold(2)
        direction(1)
        evac(3)
        turn_v(1, 1)
        fold(3)
        direction(2)
        for k in (5, 6):
            for q in range(NQ):
                mm1(k, q)
        direction(3)
        evac(4)
        evac(5)
        fold(4)
        for q in range(NQ):
            mm1(7, q)
        ileave_d(0, 0, nc.scalar.copy)
        evac(6)
        fold(5)
        direction(4)
        ileave_d(0, 1, nc.scalar.copy)
        evac(7)
        fold(6)
        direction(5)
        quant_d(0, 0)
        ileave_d(0, 2, nc.scalar.copy)
        fold(7)
        direction(6)
        quant_d(0, 1)
        ileave_d(0, 3, nc.scalar.copy)
        direction(7, slice(0, HALF))
        quant_d(0, 2)
        ileave_d(1, 0, nc.vector.tensor_copy)
        ileave_d(1, 1, nc.scalar.copy)
        direction(7, slice(HALF, DI))
        quant_d(0, 3)
        quant_d(1, 0)
        ileave_d(1, 2, nc.vector.tensor_copy)
        ileave_d(1, 3, nc.scalar.copy)
        mm2(0, [nc.scalar.copy] * 2)
        quant_d(1, 1)
        mm2(1, [nc.scalar.copy] * 2)
        quant_d(1, 2)
        mm2(2, [nc.scalar.copy] * 2)
        quant_d(1, 3)
        mm2(3, [nc.scalar.copy, nc.vector.tensor_copy])
